import numpy as np, ml_dtypes
CORES = [89,94,345,350]
N = 4
import mx_ref
NC = 128
BF = ml_dtypes.bfloat16
def cut(t, i, w=512):
    return t[:, w * i:w * i + w]
def tile(rs):
    return np.stack(rs, axis=2).reshape(128, -1).astype(BF)
def onehot(t, r):
    own, p, b = t[:, :NC], t[:, NC:2 * NC], t[:, 2 * NC:]
    return tile([((own == r) & (p == np.arange(128)[:, None]) & (b == f)).astype(np.float32) for f in range(4)])
def setup_inputs(rng):
    def f(*shape):
        return mx_ref.flush((rng.standard_normal(shape, dtype=np.float32) * np.exp2(rng.integers(-2, 3, shape[:-1] + (1,)))).astype(BF))
    t = np.concatenate([rng.integers(0, N, (N, 1, NC)), rng.integers(0, 128, (N, 1, NC)), rng.integers(0, 4, (N, 1, NC))], axis=2)
    return {"tg": np.broadcast_to(t, (N, 128, 3 * NC)).astype(BF).copy(), "tab": f(N, 128, 4 * 512), "w": f(N, 128, 512)}
def setup_inputs_blocks(rng):
    d = setup_inputs(rng)
    for k in ("tab", "w"): d[k] = mx_ref.spread(d[k], rng, 4)
    return d
def setup_inputs_wide(rng):
    d = setup_inputs(rng)
    for k in ("tab", "w"): d[k] = mx_ref.flush((d[k].astype(np.float32) * np.exp2(rng.integers(-6, 7, (N, 1, 1))).astype(np.float32)).astype(BF))
    return d
def setup_inputs_hot(rng):
    d = setup_inputs(rng); t = d["tg"].astype(np.float32); t[:, :, :NC] = rng.integers(0, N); t[:, :, NC:2 * NC] = np.broadcast_to(rng.integers(0, 4, (N, 1, NC)), (N, 128, NC))
    d["tg"] = t.astype(BF)
    return d
def reference(tg, tab, w):
    y = np.zeros((N, 128, NC), np.float32)
    for j in range(N):
        qw = mx_ref.quantize(w[j])
        for r in range(N):
            o = mx_ref.quantize(onehot(tg[j].astype(np.float32), r))
            e = mx_ref.quantize(tile([mx_ref.matmul(mx_ref.quantize(cut(tab[r], f)), o) for f in range(4)]))
            p = mx_ref.matmul(qw, e)
            y[j] = p if r == 0 else y[j] + p
    return {"y": y}

@@ -1,0 +1,289 @@
+from concourse.bass import DstId, RemoteDMATransfer
+from concourse.mybir import dt, AluOpType, ActivationFunctionType
+
+NC = 128
+OP = AluOpType
+COPY = ActivationFunctionType.Copy
+
+SCRATCH = {
+    "ids_out": ("dram", [128, 3], "bfloat16"),
+    "ids_via": ("dram", [128, 3], "bfloat16"),
+    "ids_in": ("dram", [3, 128, 3], "bfloat16"),
+    "tgs": ("sbuf", [128, 384], "bfloat16"),
+    "kr": ("sbuf", [128, 384], "bfloat16"),
+    "kp": ("sbuf", [128, 384], "bfloat16"),
+    "fr": ("sbuf", [128, 384], "bfloat16"),
+    "fp": ("sbuf", [128, 384], "bfloat16"),
+    "u1": ("sbuf", [128, 384], "bfloat16"),
+    "u2": ("sbuf", [128, 384], "bfloat16"),
+    "u3": ("sbuf", [128, 384], "bfloat16"),
+    "gk": ("sbuf", [128, 384], "bfloat16"),
+    "rep": ("sbuf", [128, 384], "bfloat16"),
+    "msk": ("sbuf", [128, 128], "bfloat16"),
+    "pc": ("sbuf", [128, 4], "bfloat16"),
+    "kab": ("sbuf", [128, 256], "bfloat16"),
+    "kown": ("sbuf", [128, 256], "bfloat16"),
+    "tabs": ("sbuf", [128, 2048], "bfloat16"),
+    "ws": ("sbuf", [128, 512], "bfloat16"),
+    "oab": ("sbuf", [128, 1024], "bfloat16"),
+    "oown": ("sbuf", [128, 1024], "bfloat16"),
+    "eab": ("sbuf", [128, 1024], "bfloat16"),
+    "eown": ("sbuf", [128, 1024], "bfloat16"),
+    "ys": ("sbuf", [128, 128], "float32"),
+    "tabq": ("sbuf", [128, 512], "float8_e4m3fn_x4"), "tabp": ("sbuf", [128, 512], "uint8"),
+    "wq": ("sbuf", [128, 128], "float8_e4m3fn_x4"), "wp": ("sbuf", [128, 128], "uint8"),
+    "oabq": ("sbuf", [128, 256], "float8_e4m3fn_x4"), "oabp": ("sbuf", [128, 256], "uint8"),
+    "oownq": ("sbuf", [128, 256], "float8_e4m3fn_x4"), "oownp": ("sbuf", [128, 256], "uint8"),
+    "eabq": ("sbuf", [128, 256], "float8_e4m3fn_x4"), "eabp": ("sbuf", [128, 256], "uint8"),
+    "eownq": ("sbuf", [128, 256], "float8_e4m3fn_x4"), "eownp": ("sbuf", [128, 256], "uint8"),
+    "lq": ("sbuf", [128, 384], "float8_e4m3fn_x4"), "lp": ("sbuf", [128, 384], "uint8"),
+    "viaq": ("sbuf", [128, 128], "float8_e4m3fn_x4"), "viap": ("sbuf", [128, 128], "uint8"),
+    "z": ("psum", [128, 4096], "float32"),
+}
+SEMAPHORES = [
+    "l_ids", "l_tg", "l_tab0", "l_tab1", "l_w", "l_kp", "l_kr", "sent",
+    "a_id0", "a_id1", "a_id2", "a_e0", "a_e1", "a_e2", "h_ids", "h_pl", "h_co",
+    "pc", "m_k", "m_1", "m_g", "m_m", "q_tab", "q_w", "kown", "o_own", "q_oown",
+    "zown", "e_own", "q_eown", "o_a", "o_b", "q_oa", "q_ob",
+    "za0", "za1", "za2", "za3", "zb0", "zb1", "zb2", "zb3",
+    "e_a", "e_bs", "e_bv", "q_ea", "q_eb", "yz", "yv", "stored",
+    "w1", "w2", "w3",
+] + ["%s%d" % (n, k) for n in ("tp", "tr") for k in range(7)]
+
+_PLAN = {}
+
+
+def relays(T, topo):
+    if _PLAN:
+        return _PLAN
+    taken = set(T.cores)
+    for r in T.cores:
+        for j in T.cores:
+            if r == j or topo.may_write(r, j):
+                continue
+            switch_first = topo.die(r) == topo.die(j)
+            for c in range(4 * topo.CORES_PER_HOST):
+                if c in taken or topo.chip(c) != topo.chip(r) or topo.die(c) != topo.die(r):
+                    continue
+                if topo.host(c) in (topo.host(r), topo.host(j)):
+                    continue
+                if not (topo.may_write(r, c) and topo.may_write(c, j)):
+                    continue
+                if topo.same_plane(r, c) != switch_first:
+                    continue
+                _PLAN[(r, j)] = c
+                taken.add(c)
+                break
+    return _PLAN
+
+
+def engines(mask):
+    return [1 << k for k in range(16) if mask & (1 << k)]
+
+
+def diagonal(T, topo, core):
+    return [c for c in T.cores if c != core and not topo.may_write(c, core)]
+
+
+def rank_program(g, core, T, topo):
+    plan = relays(T, topo)
+    if T.rank_of(core) is not None:
+        owner_program(g, core, T, topo, plan)
+        return
+    for (r, j), c in plan.items():
+        if c == core:
+            relay_program(g, core, T, topo, r, j)
+
+
+def relay_program(g, core, T, topo, r, j):
+    s = T.sem
+    slot = diagonal(T, topo, j).index(r)
+    rid, pid = topo.addr(j, core)
+    full = topo.mask(core, j)
+    eng = engines(full)
+    half = len(engines(topo.mask(r, core))) // 2
+    cols = slice(slot * NC, slot * NC + NC)
+    g.wait_ge(s.h_ids, 1)
+    g.remote_dma(T.ids_in[slot], T.ids_via[:], s["a_id%d" % slot], s.sent, pid, rid, eng[0])
+    g.wait_ge(s.h_pl, half)
+    g.remote_dma(T.lp[:, cols], T.viap[:], s["a_e%d" % slot], s.sent, pid, rid, full)
+    g.wait_ge(s.h_co, half)
+    g.remote_dma(T.lq[:, cols].bitcast(dt.uint8), T.viaq[:].bitcast(dt.uint8), s["a_e%d" % slot], s.sent, pid, rid, full)
+    g.wait_ge(s.sent, 1 + 2 * len(eng))
+
+
+def owner_program(g, core, T, topo, plan):
+    s = T.sem
+    V, A, P, S = g.vector, g.scalar, g.tensor, g.sync
+    rank = T.rank_of(core)
+    diag = diagonal(T, topo, core)
+    peer = [c for c in T.cores if c != core and c not in diag][0]
+    via = [plan[(core, d)] for d in diag]
+    off = topo.mask(core, via[0]) & topo.mask(core, via[1])
+    on = topo.mask(core, peer)
+    eng = engines(off)
+    part = [sum(eng[0::2]), sum(eng[1::2])]
+    dst = []
+    for c in via:
+        rid, pid = topo.addr(c, core)
+        dst.append(DstId(rid=rid, pnc=pid))
+    prid, ppid = topo.addr(peer, core)
+    half, n_off, n_on = len(eng) // 2, len(eng), len(engines(on))
+
+    S.dma_start(T.ids_out[:], T.tg[0:1, :]).then_inc(s.l_ids, 16)
+    A.dma_start(T.tgs[:], T.tg[:, :]).then_inc(s.l_tg, 16)
+    S.dma_start(T.tabs[:, 0:1024], T.tab[:, 0:1024]).then_inc(s.l_tab0, 16)
+    A.dma_start(T.tabs[:, 1024:2048], T.tab[:, 1024:2048]).then_inc(s.l_tab1, 16)
+    S.dma_start(T.ws[:], T.w[:, :]).then_inc(s.l_w, 16)
+
+    g.iota(T.pc[:], [[128, 4]], -256, 1, allow_small_or_imprecise_dtypes=True).then_inc(s.pc, 1)
+    g.wait_ge(s.l_ids, 16)
+    g.remote_dma_fused([RemoteDMATransfer(dst_ids=dst, dma_engine_mask=eng[0], remote_sem=s.h_ids,
+                                          srcs=[T.ids_out[:]], dsts=[T.ids_via[:], T.ids_via[:]])], local_sem=s.sent)
+    g.remote_dma(T.ids_in[2], T.ids_out[:], s.a_id2, s.sent, ppid, prid, off)
+
+    S.wait_ge(s.m_k, 2)
+    S.wait_ge(s.a_id2, n_off)
+    for a in range(4):
+        S.dma_start(T.kp[32 * a:32 * a + 1, :], T.ids_in[2]).then_inc(s.l_kp, 16)
+    A.wait_ge(s.m_k, 2)
+    for q, aa in ((S, (0, 1)), (A, (2, 3))):
+        q.wait_ge(s.a_id0, 1)
+        q.wait_ge(s.a_id1, 1)
+        for a in aa:
+            q.dma_start(T.kr[32 * a:32 * a + 2, :], T.ids_in[0:2]).then_inc(s.l_kr, 16)
+
+    V.memset(T.kp[:], 0.0).then_inc(s.m_k, 1)
+    V.memset(T.kr[:], 0.0).then_inc(s.m_k, 1)
+    V.memset(T.msk[:], 1.0).then_inc(s.m_1, 1)
+    V.memset(T.gk[:], 0.0).then_inc(s.m_g, 1)
+    V.wait_ge(s.m_1, 1)
+    V.memset(T.msk[:, 0:128:32], 0.0).then_inc(s.m_m, 1)
+    V.wait_ge(s.l_tg, 16)
+    V.tensor_scalar(T.u1[:, 256:384], T.tgs[:, 256:384], 128.0, -256.0, OP.mult, OP.add).then_inc(s.w1, 1)
+    V.tensor_scalar(T.u2[:, 256:384], T.tgs[:, 0:128], float(rank), 512.0, OP.not_equal, OP.mult).then_inc(s.w1, 1)
+    V.wait_ge(s.w1, 2)
+    V.tensor_tensor(T.u3[:, 256:384], T.u1[:, 256:384], T.tgs[:, 128:256], OP.add).then_inc(s.w2, 1)
+    V.wait_ge(s.w2, 1)
+    V.tensor_tensor(T.kown[:, 0:128], T.u3[:, 256:384], T.u2[:, 256:384], OP.add).then_inc(s.kown, 1)
+    for f in range(4):
+        if f % 2 == 0:
+            V.wait_ge(s["l_tab%d" % (f // 2)], 16)
+        V.quantize_mx(T.tabq[:, NC * f:NC * f + NC], T.tabp[:, NC * f:NC * f + NC],
+                      T.tabs[:, 512 * f:512 * f + 512]).then_inc(s.q_tab, 1)
+    V.wait_ge(s.l_w, 16)
+    V.quantize_mx(T.wq[:], T.wp[:], T.ws[:]).then_inc(s.q_w, 1)
+    V.wait_ge(s.m_g, 1)
+    V.wait_ge(s.m_m, 1)
+
+    def keys(rows, cols, base, n, out, t):
+        V.transpose(cols[:], rows[:]).then_inc(s[t + "0"], 1)
+        V.wait_ge(s[t + "0"], 1)
+        V.tensor_scalar(T.u1[:, base:base + 128], cols[:, 256:384], 128.0, -256.0, OP.mult, OP.add).then_inc(s[t + "1"], 1)
+        V.tensor_scalar(T.u2[:, base:base + 128], cols[:, 0:128], float(rank), 512.0, OP.not_equal, OP.mult).then_inc(s[t + "1"], 1)
+        V.wait_ge(s[t + "1"], 2)
+        for k in range(n):
+            V.tensor_tensor(T.u3[:, base + k:base + 128:32], T.u1[:, base + k:base + 128:32],
+                            cols[:, 128 + k:256:32], OP.add).then_inc(s[t + "2"], 1)
+        V.wait_ge(s[t + "2"], n)
+        for k in range(n):
+            b = base + 128 * k
+            V.tensor_tensor(T.gk[:, b:b + 128:32], T.u3[:, base + k:base + 128:32],
+                            T.u2[:, base + k:base + 128:32], OP.add).then_inc(s[t + "3"], 1)
+        V.wait_ge(s[t + "3"], n)
+        for k in range(n):
+            b = base + 128 * k
+            V.tensor_tensor_scan(T.rep[:, b:b + 128], T.msk[:], T.gk[:, b:b + 128], 0.0, OP.mult, OP.add).then_inc(s[t + "4"], 1)
+        V.wait_ge(s[t + "4"], n)
+        V.transpose(out, T.rep[:, base:base + 128 * n]).then_inc(s[t + "5"], 1)
+        V.wait_ge(s[t + "5"], 1)
+
+    V.wait_ge(s.l_kp, 64)
+    keys(T.kp, T.fp, 256, 1, T.kown[:, 128:256], "tp")
+    V.wait_ge(s.kown, 1)
+    V.wait_ge(s.pc, 1)
+    for f in range(4):
+        V.tensor_scalar(T.oown[:, f:1024:4], T.kown[:], T.pc[:, f:f + 1], None, OP.is_equal).then_inc(s.o_own, 1)
+    V.wait_ge(s.o_own, 4)
+    V.quantize_mx(T.oownq[:], T.oownp[:], T.oown[:]).then_inc(s.q_oown, 1)
+
+    V.wait_ge(s.l_kr, 64)
+    keys(T.kr, T.fr, 0, 2, T.kab[:], "tr")
+    for k, t in ((0, "a"), (1, "b")):
+        for f in range(4):
+            V.tensor_scalar(T.oab[:, 512 * k + f:512 * k + 512:4], T.kab[:, NC * k:NC * k + NC], T.pc[:, f:f + 1], None,
+                            OP.is_equal).then_inc(s["o_" + t], 1)
+        V.wait_ge(s["o_" + t], 4)
+        V.quantize_mx(T.oabq[:, NC * k:NC * k + NC], T.oabp[:, NC * k:NC * k + NC],
+                      T.oab[:, 512 * k:512 * k + 512]).then_inc(s["q_o" + t], 1)
+
+    P.wait_ge(s.q_tab, 4)
+    P.wait_ge(s.q_oown, 1)
+
+    def tab(f):
+        return T.tabq[:, NC * f:NC * f + NC], T.tabp[:, NC * f:NC * f + NC]
+
+    for f in range(4):
+        q, p = tab(f)
+        P.matmul_mx(T.z[:, 512 * f:512 * f + 256], q, p, T.oownq[:], T.oownp[:], True, True).then_inc(s.zown, 1)
+    P.wait_ge(s.q_oa, 1)
+    for f in range(4):
+        q, p = tab(f)
+        P.matmul_mx(T.z[:, 2048 + 512 * f:2048 + 512 * f + NC], q, p, T.oabq[:, 0:NC], T.oabp[:, 0:NC],
+                    True, True).then_inc(s["za%d" % f], 1)
+    P.wait_ge(s.e_own, 4)
+    P.wait_ge(s.q_ob, 1)
+    for f in range(4):
+        q, p = tab(f)
+        P.matmul_mx(T.z[:, 512 * f:512 * f + NC], q, p, T.oabq[:, NC:2 * NC], T.oabp[:, NC:2 * NC],
+                    True, True).then_inc(s["zb%d" % f], 1)
+
+    A.wait_ge(s.zown, 4)
+    for f in range(4):
+        A.activation(T.eown[:, f:1024:4], T.z[:, 512 * f:512 * f + 256], COPY).then_inc(s.e_own, 1)
+    for f in range(4):
+        A.wait_ge(s["za%d" % f], 1)
+        A.activation(T.eab[:, f:512:4], T.z[:, 2048 + 512 * f:2048 + 512 * f + NC], COPY).then_inc(s.e_a, 1)
+    for f in (0, 2):
+        A.wait_ge(s["zb%d" % f], 1)
+        A.activation(T.eab[:, 512 + f:1024:4], T.z[:, 512 * f:512 * f + NC], COPY).then_inc(s.e_bs, 1)
+    V.wait_ge(s.e_a, 4)
+    V.quantize_mx(T.eabq[:, 0:NC], T.eabp[:, 0:NC], T.eab[:, 0:512]).then_inc(s.q_ea, 1)
+    for f in (1, 3):
+        V.wait_ge(s["zb%d" % f], 1)
+        V.tensor_copy(T.eab[:, 512 + f:1024:4], T.z[:, 512 * f:512 * f + NC]).then_inc(s.e_bv, 1)
+    V.wait_ge(s.e_bs, 2)
+    V.wait_ge(s.e_bv, 2)
+    V.quantize_mx(T.eabq[:, NC:2 * NC], T.eabp[:, NC:2 * NC], T.eab[:, 512:1024]).then_inc(s.q_eb, 1)
+    V.wait_ge(s.e_own, 4)
+    V.quantize_mx(T.eownq[:], T.eownp[:], T.eown[:]).then_inc(s.q_eown, 1)
+
+    g.wait_ge(s.q_ea, 1)
+    g.wait_ge(s.q_eb, 1)
+    g.remote_dma_fused([RemoteDMATransfer(dst_ids=[dst[k]], dma_engine_mask=part[k], remote_sem=s.h_pl,
+                                          src=T.eabp[:, NC * k:NC * k + NC], dst=T.viap[:]) for k in range(2)],
+                       local_sem=s.sent)
+    g.remote_dma_fused([RemoteDMATransfer(dst_ids=[dst[k]], dma_engine_mask=part[k], remote_sem=s.h_co,
+                                          src=T.eabq[:, NC * k:NC * k + NC].bitcast(dt.uint8),
+                                          dst=T.viaq[:].bitcast(dt.uint8)) for k in range(2)],
+                       local_sem=s.sent)
+    g.wait_ge(s.q_eown, 1)
+    g.remote_dma(T.lp[:, 256:384], T.eownp[:, NC:2 * NC], s.a_e2, s.sent, ppid, prid, on)
+    g.remote_dma(T.lq[:, 256:384].bitcast(dt.uint8), T.eownq[:, NC:2 * NC].bitcast(dt.uint8), s.a_e2, s.sent, ppid, prid, on)
+
+    P.wait_ge(s.q_w, 1)
+    P.wait_ge(s.e_a, 4)
+    P.wait_ge(s.q_eown, 1)
+    yb = T.z[:, 2048:2048 + NC]
+    P.matmul_mx(yb, T.wq[:], T.wp[:], T.eownq[:, 0:NC], T.eownp[:, 0:NC], True, False)
+    for k, n in ((2, 2 * n_on), (0, 2 * n_off), (1, 2 * n_off)):
+        P.wait_ge(s["a_e%d" % k], n)
+        mm = P.matmul_mx(yb, T.wq[:], T.wp[:], T.lq[:, NC * k:NC * k + NC], T.lp[:, NC * k:NC * k + NC], False, k == 1)
+        if k == 1:
+            mm.then_inc(s.yz, 1)
+    V.wait_ge(s.yz, 1)
+    V.tensor_copy(T.ys[:], yb).then_inc(s.yv, 1)
+    S.wait_ge(s.yv, 1)
+    S.dma_start(T.y[:, :], T.ys[:]).then_inc(s.stored, 16)
+    S.wait_ge(s.stored, 16)
+    g.wait_ge(s.sent, 1 + n_off + 2 * half * 2 + 2 * n_on)

@@ -10,32 +10,34 @@ SCRATCH = {
     "ids_via": ("dram", [128, 3], "bfloat16"),
     "ids_in": ("dram", [3, 128, 3], "bfloat16"),
     "tgs": ("sbuf", [128, 384], "bfloat16"),
-    "kr": ("sbuf", [128, 384], "bfloat16"),
-    "kp": ("sbuf", [128, 384], "bfloat16"),
-    "fr": ("sbuf", [128, 384], "bfloat16"),
-    "fp": ("sbuf", [128, 384], "bfloat16"),
-    "u1": ("sbuf", [128, 384], "bfloat16"),
-    "u2": ("sbuf", [128, 384], "bfloat16"),
-    "u3": ("sbuf", [128, 384], "bfloat16"),
+    "kr": ("sbuf", [128, 128], "bfloat16"),
+    "kp": ("sbuf", [128, 128], "bfloat16"),
+    "fr": ("sbuf", [128, 128], "bfloat16"),
+    "fp": ("sbuf", [128, 128], "bfloat16"),
+    "sr": ("sbuf", [128, 128], "float32"),
+    "sp": ("sbuf", [128, 128], "float32"),
+    "cf": ("sbuf", [128, 128], "bfloat16"),
     "gk": ("sbuf", [128, 384], "bfloat16"),
     "rep": ("sbuf", [128, 384], "bfloat16"),
-    "msk": ("sbuf", [128, 128], "bfloat16"),
+    "msk": ("sbuf", [128, 256], "bfloat16"),
+    "u1": ("sbuf", [128, 128], "float32"),
+    "u2": ("sbuf", [128, 128], "float32"),
+    "u3": ("sbuf", [128, 128], "float32"),
     "pc": ("sbuf", [128, 4], "bfloat16"),
     "kab": ("sbuf", [128, 256], "bfloat16"),
-    "kown": ("sbuf", [128, 256], "bfloat16"),
+    "kpe": ("sbuf", [128, 128], "bfloat16"),
+    "kown": ("sbuf", [128, 128], "bfloat16"),
     "tabs": ("sbuf", [128, 2048], "bfloat16"),
     "ws": ("sbuf", [128, 512], "bfloat16"),
-    "oab": ("sbuf", [128, 1024], "bfloat16"),
-    "oown": ("sbuf", [128, 1024], "bfloat16"),
-    "eab": ("sbuf", [128, 1024], "bfloat16"),
-    "eown": ("sbuf", [128, 1024], "bfloat16"),
+    "oa": ("sbuf", [128, 512], "bfloat16"), "ob": ("sbuf", [128, 512], "bfloat16"),
+    "oo": ("sbuf", [128, 512], "bfloat16"), "op": ("sbuf", [128, 512], "bfloat16"),
+    "ea": ("sbuf", [128, 512], "bfloat16"), "eb": ("sbuf", [128, 512], "bfloat16"),
+    "eo": ("sbuf", [128, 512], "bfloat16"), "ep": ("sbuf", [128, 512], "bfloat16"),
     "ys": ("sbuf", [128, 128], "float32"),
     "tabq": ("sbuf", [128, 512], "float8_e4m3fn_x4"), "tabp": ("sbuf", [128, 512], "uint8"),
     "wq": ("sbuf", [128, 128], "float8_e4m3fn_x4"), "wp": ("sbuf", [128, 128], "uint8"),
-    "oabq": ("sbuf", [128, 256], "float8_e4m3fn_x4"), "oabp": ("sbuf", [128, 256], "uint8"),
-    "oownq": ("sbuf", [128, 256], "float8_e4m3fn_x4"), "oownp": ("sbuf", [128, 256], "uint8"),
-    "eabq": ("sbuf", [128, 256], "float8_e4m3fn_x4"), "eabp": ("sbuf", [128, 256], "uint8"),
-    "eownq": ("sbuf", [128, 256], "float8_e4m3fn_x4"), "eownp": ("sbuf", [128, 256], "uint8"),
+    "oq": ("sbuf", [128, 512], "float8_e4m3fn_x4"), "opl": ("sbuf", [128, 512], "uint8"),
+    "eq": ("sbuf", [128, 512], "float8_e4m3fn_x4"), "epl": ("sbuf", [128, 512], "uint8"),
     "lq": ("sbuf", [128, 384], "float8_e4m3fn_x4"), "lp": ("sbuf", [128, 384], "uint8"),
     "viaq": ("sbuf", [128, 128], "float8_e4m3fn_x4"), "viap": ("sbuf", [128, 128], "uint8"),
     "z": ("psum", [128, 4096], "float32"),
@@ -43,14 +45,13 @@ SCRATCH = {
 SEMAPHORES = [
     "l_ids", "l_tg", "l_tab0", "l_tab1", "l_w", "l_kp", "l_kr", "sent",
     "a_id0", "a_id1", "a_id2", "a_e0", "a_e1", "a_e2", "h_ids", "h_pl", "h_co",
-    "pc", "m_k", "m_1", "m_g", "m_m", "q_tab", "q_w", "kown", "o_own", "q_oown",
-    "zown", "e_own", "q_eown", "o_a", "o_b", "q_oa", "q_ob",
-    "za0", "za1", "za2", "za3", "zb0", "zb1", "zb2", "zb3",
-    "e_a", "e_bs", "e_bv", "q_ea", "q_eb", "yz", "yv", "stored",
-    "w1", "w2", "w3",
-] + ["%s%d" % (n, k) for n in ("tp", "tr") for k in range(7)]
+    "pc", "m_k", "m_1", "m_g", "m_m", "m_c", "m_cf", "q_tab", "q_w", "kown", "yz", "yv", "stored", "w1", "w2",
+] + ["%s%d" % (n, k) for n in ("tp", "tr") for k in range(5)] \
+  + [n + t for t in "abop" for n in ("o_", "qo_", "es_", "ev_", "qe_")] \
+  + ["z%s%d" % (t, f) for t in "abop" for f in range(4)]
 
 _PLAN = {}
+COL = {"a": 0, "b": 1, "o": 2, "p": 3}
 
 
 def relays(T, topo):
@@ -101,14 +102,14 @@ def relay_program(g, core, T, topo, r, j):
     rid, pid = topo.addr(j, core)
     full = topo.mask(core, j)
     eng = engines(full)
-    half = len(engines(topo.mask(r, core))) // 2
+    n_in = len(engines(topo.mask(r, core)))
     cols = slice(slot * NC, slot * NC + NC)
     g.wait_ge(s.h_ids, 1)
     g.remote_dma(T.ids_in[slot], T.ids_via[:], s["a_id%d" % slot], s.sent, pid, rid, eng[0])
-    g.wait_ge(s.h_pl, half)
-    g.remote_dma(T.lp[:, cols], T.viap[:], s["a_e%d" % slot], s.sent, pid, rid, full)
-    g.wait_ge(s.h_co, half)
+    g.wait_ge(s.h_co, n_in)
     g.remote_dma(T.lq[:, cols].bitcast(dt.uint8), T.viaq[:].bitcast(dt.uint8), s["a_e%d" % slot], s.sent, pid, rid, full)
+    g.wait_ge(s.h_pl, n_in // 2)
+    g.remote_dma(T.lp[:, cols], T.viap[:], s["a_e%d" % slot], s.sent, pid, rid, full)
     g.wait_ge(s.sent, 1 + 2 * len(eng))
 
 
@@ -116,11 +117,12 @@ def owner_program(g, core, T, topo, plan):
     s = T.sem
     V, A, P, S = g.vector, g.scalar, g.tensor, g.sync
     rank = T.rank_of(core)
+    shift = -1024.0 * rank - 256.0
     diag = diagonal(T, topo, core)
     peer = [c for c in T.cores if c != core and c not in diag][0]
-    via = [plan[(core, d)] for d in diag]
+    slot = sorted(range(2), key=lambda k: 0 if topo.same_plane(core, plan[(core, diag[k])]) else 1)
+    via = [plan[(core, diag[k])] for k in slot]
     off = topo.mask(core, via[0]) & topo.mask(core, via[1])
-    on = topo.mask(core, peer)
     eng = engines(off)
     part = [sum(eng[0::2]), sum(eng[1::2])]
     dst = []
@@ -128,7 +130,10 @@ def owner_program(g, core, T, topo, plan):
         rid, pid = topo.addr(c, core)
         dst.append(DstId(rid=rid, pnc=pid))
     prid, ppid = topo.addr(peer, core)
-    half, n_off, n_on = len(eng) // 2, len(eng), len(engines(on))
+    n_off = len(eng)
+
+    def blk(t):
+        return slice(NC * COL[t], NC * COL[t] + NC)
 
     S.dma_start(T.ids_out[:], T.tg[0:1, :]).then_inc(s.l_ids, 16)
     A.dma_start(T.tgs[:], T.tg[:, :]).then_inc(s.l_tg, 16)
@@ -136,36 +141,49 @@ def owner_program(g, core, T, topo, plan):
     A.dma_start(T.tabs[:, 1024:2048], T.tab[:, 1024:2048]).then_inc(s.l_tab1, 16)
     S.dma_start(T.ws[:], T.w[:, :]).then_inc(s.l_w, 16)
 
-    g.iota(T.pc[:], [[128, 4]], -256, 1, allow_small_or_imprecise_dtypes=True).then_inc(s.pc, 1)
+    g.iota(T.pc[:], [[1, 4]], -256, 4, allow_small_or_imprecise_dtypes=True).then_inc(s.pc, 1)
     g.wait_ge(s.l_ids, 16)
     g.remote_dma_fused([RemoteDMATransfer(dst_ids=dst, dma_engine_mask=eng[0], remote_sem=s.h_ids,
                                           srcs=[T.ids_out[:]], dsts=[T.ids_via[:], T.ids_via[:]])], local_sem=s.sent)
     g.remote_dma(T.ids_in[2], T.ids_out[:], s.a_id2, s.sent, ppid, prid, off)
 
-    S.wait_ge(s.m_k, 2)
-    S.wait_ge(s.a_id2, n_off)
-    for a in range(4):
-        S.dma_start(T.kp[32 * a:32 * a + 1, :], T.ids_in[2]).then_inc(s.l_kp, 16)
-    A.wait_ge(s.m_k, 2)
     for q, aa in ((S, (0, 1)), (A, (2, 3))):
+        q.wait_ge(s.m_k, 2)
         q.wait_ge(s.a_id0, 1)
         q.wait_ge(s.a_id1, 1)
         for a in aa:
-            q.dma_start(T.kr[32 * a:32 * a + 2, :], T.ids_in[0:2]).then_inc(s.l_kr, 16)
+            q.dma_start(T.kr[32 * a:32 * a + 6, :], T.ids_in[0:2]).then_inc(s.l_kr, 16)
+    S.wait_ge(s.a_id2, n_off)
+    for a in range(4):
+        S.dma_start(T.kp[32 * a:32 * a + 3, :], T.ids_in[2]).then_inc(s.l_kp, 16)
 
-    V.memset(T.kp[:], 0.0).then_inc(s.m_k, 1)
     V.memset(T.kr[:], 0.0).then_inc(s.m_k, 1)
+    V.memset(T.kp[:], 0.0).then_inc(s.m_k, 1)
+    V.memset(T.cf[:], 0.0).then_inc(s.m_c, 1)
     V.memset(T.msk[:], 1.0).then_inc(s.m_1, 1)
     V.memset(T.gk[:], 0.0).then_inc(s.m_g, 1)
+    V.wait_ge(s.m_c, 1)
+    for c0, v in ((1, 256.0), (2, 4.0), (4, 256.0), (5, 4.0)):
+        V.memset(T.cf[:, c0:128:32], v).then_inc(s.m_cf, 1)
     V.wait_ge(s.m_1, 1)
-    V.memset(T.msk[:, 0:128:32], 0.0).then_inc(s.m_m, 1)
+    V.memset(T.msk[:, 0:256:32], 0.0).then_inc(s.m_m, 1)
     V.wait_ge(s.l_tg, 16)
-    V.tensor_scalar(T.u1[:, 256:384], T.tgs[:, 256:384], 128.0, -256.0, OP.mult, OP.add).then_inc(s.w1, 1)
-    V.tensor_scalar(T.u2[:, 256:384], T.tgs[:, 0:128], float(rank), 512.0, OP.not_equal, OP.mult).then_inc(s.w1, 1)
+    V.tensor_scalar(T.u1[:], T.tgs[:, 0:128], 1024.0, shift, OP.mult, OP.add).then_inc(s.w1, 1)
+    V.tensor_scalar(T.u2[:], T.tgs[:, 128:256], 4.0, None, OP.mult).then_inc(s.w1, 1)
     V.wait_ge(s.w1, 2)
-    V.tensor_tensor(T.u3[:, 256:384], T.u1[:, 256:384], T.tgs[:, 128:256], OP.add).then_inc(s.w2, 1)
+    V.tensor_tensor(T.u3[:], T.u2[:], T.tgs[:, 256:384], OP.add).then_inc(s.w2, 1)
     V.wait_ge(s.w2, 1)
-    V.tensor_tensor(T.kown[:, 0:128], T.u3[:, 256:384], T.u2[:, 256:384], OP.add).then_inc(s.kown, 1)
+    V.tensor_tensor(T.kown[:], T.u3[:], T.u1[:], OP.add).then_inc(s.kown, 1)
+    V.wait_ge(s.kown, 1)
+    V.wait_ge(s.pc, 1)
+
+    def onehot(t, tile, key):
+        for f in range(4):
+            V.tensor_scalar(tile[:, f:512:4], key, T.pc[:, f:f + 1], None, OP.is_equal).then_inc(s["o_" + t], 1)
+        V.wait_ge(s["o_" + t], 4)
+        V.quantize_mx(T.oq[:, blk(t)], T.opl[:, blk(t)], tile[:]).then_inc(s["qo_" + t], 1)
+
+    onehot("o", T.oo, T.kown[:])
     for f in range(4):
         if f % 2 == 0:
             V.wait_ge(s["l_tab%d" % (f // 2)], 16)
@@ -175,115 +193,98 @@ def owner_program(g, core, T, topo, plan):
     V.quantize_mx(T.wq[:], T.wp[:], T.ws[:]).then_inc(s.q_w, 1)
     V.wait_ge(s.m_g, 1)
     V.wait_ge(s.m_m, 1)
+    V.wait_ge(s.m_cf, 4)
 
-    def keys(rows, cols, base, n, out, t):
+    def keys(rows, cols, sc, base, n, out, t):
         V.transpose(cols[:], rows[:]).then_inc(s[t + "0"], 1)
         V.wait_ge(s[t + "0"], 1)
-        V.tensor_scalar(T.u1[:, base:base + 128], cols[:, 256:384], 128.0, -256.0, OP.mult, OP.add).then_inc(s[t + "1"], 1)
-        V.tensor_scalar(T.u2[:, base:base + 128], cols[:, 0:128], float(rank), 512.0, OP.not_equal, OP.mult).then_inc(s[t + "1"], 1)
-        V.wait_ge(s[t + "1"], 2)
+        V.tensor_tensor_scan(sc[:], T.cf[:], cols[:], 0.0, OP.mult, OP.add).then_inc(s[t + "1"], 1)
+        V.wait_ge(s[t + "1"], 1)
         for k in range(n):
-            V.tensor_tensor(T.u3[:, base + k:base + 128:32], T.u1[:, base + k:base + 128:32],
-                            cols[:, 128 + k:256:32], OP.add).then_inc(s[t + "2"], 1)
+            b = base + 128 * k
+            V.tensor_scalar(T.gk[:, b:b + 128:32], sc[:, 3 * k + 2:128:32], shift, None, OP.add).then_inc(s[t + "2"], 1)
         V.wait_ge(s[t + "2"], n)
-        for k in range(n):
-            b = base + 128 * k
-            V.tensor_tensor(T.gk[:, b:b + 128:32], T.u3[:, base + k:base + 128:32],
-                            T.u2[:, base + k:base + 128:32], OP.add).then_inc(s[t + "3"], 1)
-        V.wait_ge(s[t + "3"], n)
-        for k in range(n):
-            b = base + 128 * k
-            V.tensor_tensor_scan(T.rep[:, b:b + 128], T.msk[:], T.gk[:, b:b + 128], 0.0, OP.mult, OP.add).then_inc(s[t + "4"], 1)
-        V.wait_ge(s[t + "4"], n)
-        V.transpose(out, T.rep[:, base:base + 128 * n]).then_inc(s[t + "5"], 1)
-        V.wait_ge(s[t + "5"], 1)
+        V.tensor_tensor_scan(T.rep[:, base:base + 128 * n], T.msk[:, 0:128 * n], T.gk[:, base:base + 128 * n], 0.0,
+                             OP.mult, OP.add).then_inc(s[t + "3"], 1)
+        V.wait_ge(s[t + "3"], 1)
+        V.transpose(out[:], T.rep[:, base:base + 128 * n]).then_inc(s[t + "4"], 1)
+        V.wait_ge(s[t + "4"], 1)
 
-    V.wait_ge(s.l_kp, 64)
-    keys(T.kp, T.fp, 256, 1, T.kown[:, 128:256], "tp")
-    V.wait_ge(s.kown, 1)
-    V.wait_ge(s.pc, 1)
-    for f in range(4):
-        V.tensor_scalar(T.oown[:, f:1024:4], T.kown[:], T.pc[:, f:f + 1], None, OP.is_equal).then_inc(s.o_own, 1)
-    V.wait_ge(s.o_own, 4)
-    V.quantize_mx(T.oownq[:], T.oownp[:], T.oown[:]).then_inc(s.q_oown, 1)
+    def zbank(t, f):
+        b = 512 * f + (0 if t in "ap" else 2048)
+        return T.z[:, b:b + NC]
+
+    def out_of_psum(t, tile, ff, on_vector):
+        for f in ff:
+            if on_vector:
+                V.wait_ge(s["z%s%d" % (t, f)], 1)
+                V.tensor_copy(tile[:, f:512:4], zbank(t, f)).then_inc(s["ev_" + t], 1)
+            else:
+                A.wait_ge(s["z%s%d" % (t, f)], 1)
+                A.activation(tile[:, f:512:4], zbank(t, f), COPY).then_inc(s["es_" + t], 1)
+
+    def copied(q, t):
+        n_s = {"a": 3, "b": 2, "o": 4, "p": 2}[t]
+        q.wait_ge(s["es_" + t], n_s)
+        if n_s < 4:
+            q.wait_ge(s["ev_" + t], 4 - n_s)
+
+    def codes(t, tile):
+        copied(V, t)
+        V.quantize_mx(T.eq[:, blk(t)], T.epl[:, blk(t)], tile[:]).then_inc(s["qe_" + t], 1)
 
     V.wait_ge(s.l_kr, 64)
-    keys(T.kr, T.fr, 0, 2, T.kab[:], "tr")
-    for k, t in ((0, "a"), (1, "b")):
-        for f in range(4):
-            V.tensor_scalar(T.oab[:, 512 * k + f:512 * k + 512:4], T.kab[:, NC * k:NC * k + NC], T.pc[:, f:f + 1], None,
-                            OP.is_equal).then_inc(s["o_" + t], 1)
-        V.wait_ge(s["o_" + t], 4)
-        V.quantize_mx(T.oabq[:, NC * k:NC * k + NC], T.oabp[:, NC * k:NC * k + NC],
-                      T.oab[:, 512 * k:512 * k + 512]).then_inc(s["q_o" + t], 1)
+    keys(T.kr, T.fr, T.sr, 0, 2, T.kab, "tr")
+    onehot("a", T.oa, T.kab[:, NC * slot[0]:NC * slot[0] + NC])
+    onehot("b", T.ob, T.kab[:, NC * slot[1]:NC * slot[1] + NC])
+    out_of_psum("a", T.ea, (3,), True)
+    codes("a", T.ea)
+    out_of_psum("b", T.eb, (1, 3), True)
+    codes("b", T.eb)
+    V.wait_ge(s.l_kp, 64)
+    keys(T.kp, T.fp, T.sp, 256, 1, T.kpe, "tp")
+    onehot("p", T.op, T.kpe[:])
+    codes("o", T.eo)
+    out_of_psum("p", T.ep, (1, 3), True)
+    codes("p", T.ep)
+
+    out_of_psum("o", T.eo, (0, 1, 2, 3), False)
+    out_of_psum("a", T.ea, (0, 1, 2), False)
+    out_of_psum("b", T.eb, (0, 2), False)
+    out_of_psum("p", T.ep, (0, 2), False)
 
     P.wait_ge(s.q_tab, 4)
-    P.wait_ge(s.q_oown, 1)
+    for t, before in (("o", None), ("a", None), ("b", "o"), ("p", "a")):
+        if before:
+            copied(P, before)
+        P.wait_ge(s["qo_" + t], 1)
+        for f in range(4):
+            P.matmul_mx(zbank(t, f), T.tabq[:, NC * f:NC * f + NC], T.tabp[:, NC * f:NC * f + NC],
+                        T.oq[:, blk(t)], T.opl[:, blk(t)], True, True).then_inc(s["z%s%d" % (t, f)], 1)
 
-    def tab(f):
-        return T.tabq[:, NC * f:NC * f + NC], T.tabp[:, NC * f:NC * f + NC]
-
-    for f in range(4):
-        q, p = tab(f)
-        P.matmul_mx(T.z[:, 512 * f:512 * f + 256], q, p, T.oownq[:], T.oownp[:], True, True).then_inc(s.zown, 1)
-    P.wait_ge(s.q_oa, 1)
-    for f in range(4):
-        q, p = tab(f)
-        P.matmul_mx(T.z[:, 2048 + 512 * f:2048 + 512 * f + NC], q, p, T.oabq[:, 0:NC], T.oabp[:, 0:NC],
-                    True, True).then_inc(s["za%d" % f], 1)
-    P.wait_ge(s.e_own, 4)
-    P.wait_ge(s.q_ob, 1)
-    for f in range(4):
-        q, p = tab(f)
-        P.matmul_mx(T.z[:, 512 * f:512 * f + NC], q, p, T.oabq[:, NC:2 * NC], T.oabp[:, NC:2 * NC],
-                    True, True).then_inc(s["zb%d" % f], 1)
-
-    A.wait_ge(s.zown, 4)
-    for f in range(4):
-        A.activation(T.eown[:, f:1024:4], T.z[:, 512 * f:512 * f + 256], COPY).then_inc(s.e_own, 1)
-    for f in range(4):
-        A.wait_ge(s["za%d" % f], 1)
-        A.activation(T.eab[:, f:512:4], T.z[:, 2048 + 512 * f:2048 + 512 * f + NC], COPY).then_inc(s.e_a, 1)
-    for f in (0, 2):
-        A.wait_ge(s["zb%d" % f], 1)
-        A.activation(T.eab[:, 512 + f:1024:4], T.z[:, 512 * f:512 * f + NC], COPY).then_inc(s.e_bs, 1)
-    V.wait_ge(s.e_a, 4)
-    V.quantize_mx(T.eabq[:, 0:NC], T.eabp[:, 0:NC], T.eab[:, 0:512]).then_inc(s.q_ea, 1)
-    for f in (1, 3):
-        V.wait_ge(s["zb%d" % f], 1)
-        V.tensor_copy(T.eab[:, 512 + f:1024:4], T.z[:, 512 * f:512 * f + NC]).then_inc(s.e_bv, 1)
-    V.wait_ge(s.e_bs, 2)
-    V.wait_ge(s.e_bv, 2)
-    V.quantize_mx(T.eabq[:, NC:2 * NC], T.eabp[:, NC:2 * NC], T.eab[:, 512:1024]).then_inc(s.q_eb, 1)
-    V.wait_ge(s.e_own, 4)
-    V.quantize_mx(T.eownq[:], T.eownp[:], T.eown[:]).then_inc(s.q_eown, 1)
-
-    g.wait_ge(s.q_ea, 1)
-    g.wait_ge(s.q_eb, 1)
+    for k, t in ((0, "a"), (1, "b")):
+        g.wait_ge(s["qe_" + t], 1)
+        g.remote_dma(T.viaq[:].bitcast(dt.uint8), T.eq[:, blk(t)].bitcast(dt.uint8), s.h_co, s.sent, dst[k].pnc, dst[k].rid, off)
     g.remote_dma_fused([RemoteDMATransfer(dst_ids=[dst[k]], dma_engine_mask=part[k], remote_sem=s.h_pl,
-                                          src=T.eabp[:, NC * k:NC * k + NC], dst=T.viap[:]) for k in range(2)],
+                                          src=T.epl[:, blk(t)], dst=T.viap[:]) for k, t in ((0, "a"), (1, "b"))],
                        local_sem=s.sent)
-    g.remote_dma_fused([RemoteDMATransfer(dst_ids=[dst[k]], dma_engine_mask=part[k], remote_sem=s.h_co,
-                                          src=T.eabq[:, NC * k:NC * k + NC].bitcast(dt.uint8),
-                                          dst=T.viaq[:].bitcast(dt.uint8)) for k in range(2)],
-                       local_sem=s.sent)
-    g.wait_ge(s.q_eown, 1)
-    g.remote_dma(T.lp[:, 256:384], T.eownp[:, NC:2 * NC], s.a_e2, s.sent, ppid, prid, on)
-    g.remote_dma(T.lq[:, 256:384].bitcast(dt.uint8), T.eownq[:, NC:2 * NC].bitcast(dt.uint8), s.a_e2, s.sent, ppid, prid, on)
+    g.wait_ge(s.qe_p, 1)
+    g.remote_dma(T.lq[:, 256:384].bitcast(dt.uint8), T.eq[:, blk("p")].bitcast(dt.uint8), s.a_e2, s.sent, ppid, prid, off)
+    g.remote_dma(T.lp[:, 256:384], T.epl[:, blk("p")], s.a_e2, s.sent, ppid, prid, off)
 
     P.wait_ge(s.q_w, 1)
-    P.wait_ge(s.e_a, 4)
-    P.wait_ge(s.q_eown, 1)
-    yb = T.z[:, 2048:2048 + NC]
-    P.matmul_mx(yb, T.wq[:], T.wp[:], T.eownq[:, 0:NC], T.eownp[:, 0:NC], True, False)
-    for k, n in ((2, 2 * n_on), (0, 2 * n_off), (1, 2 * n_off)):
-        P.wait_ge(s["a_e%d" % k], n)
-        mm = P.matmul_mx(yb, T.wq[:], T.wp[:], T.lq[:, NC * k:NC * k + NC], T.lp[:, NC * k:NC * k + NC], False, k == 1)
-        if k == 1:
+    copied(P, "b")
+    P.wait_ge(s.qe_o, 1)
+    yb = zbank("b", 0)
+    P.matmul_mx(yb, T.wq[:], T.wp[:], T.eq[:, blk("o")], T.epl[:, blk("o")], True, False)
+    for k in (2, slot[0], slot[1]):
+        P.wait_ge(s["a_e%d" % k], 2 * n_off)
+        mm = P.matmul_mx(yb, T.wq[:], T.wp[:], T.lq[:, NC * k:NC * k + NC], T.lp[:, NC * k:NC * k + NC], False, k == slot[1])
+        if k == slot[1]:
             mm.then_inc(s.yz, 1)
     V.wait_ge(s.yz, 1)
     V.tensor_copy(T.ys[:], yb).then_inc(s.yv, 1)
     S.wait_ge(s.yv, 1)
     S.dma_start(T.y[:, :], T.ys[:]).then_inc(s.stored, 16)
     S.wait_ge(s.stored, 16)
-    g.wait_ge(s.sent, 1 + n_off + 2 * half * 2 + 2 * n_on)
+    g.wait_ge(s.sent, 1 + n_off + 2 * n_off + n_off + 2 * n_off)

from concourse.bass import DstId, RemoteDMATransfer
from concourse.mybir import dt, AluOpType, ActivationFunctionType

NC = 128
OP = AluOpType
COPY = ActivationFunctionType.Copy

SCRATCH = {
    "ids_out": ("dram", [128, 3], "bfloat16"),
    "ids_via": ("dram", [128, 3], "bfloat16"),
    "ids_in": ("dram", [3, 128, 3], "bfloat16"),
    "tgs": ("sbuf", [128, 384], "bfloat16"),
    "kr": ("sbuf", [128, 128], "bfloat16"),
    "kp": ("sbuf", [128, 128], "bfloat16"),
    "fr": ("sbuf", [128, 128], "bfloat16"),
    "fp": ("sbuf", [128, 128], "bfloat16"),
    "sr": ("sbuf", [128, 128], "float32"),
    "sp": ("sbuf", [128, 128], "float32"),
    "cf": ("sbuf", [128, 128], "bfloat16"),
    "gk": ("sbuf", [128, 384], "bfloat16"),
    "rep": ("sbuf", [128, 384], "bfloat16"),
    "msk": ("sbuf", [128, 256], "bfloat16"),
    "u1": ("sbuf", [128, 128], "float32"),
    "u2": ("sbuf", [128, 128], "float32"),
    "u3": ("sbuf", [128, 128], "float32"),
    "pc": ("sbuf", [128, 4], "bfloat16"),
    "kab": ("sbuf", [128, 256], "bfloat16"),
    "kpe": ("sbuf", [128, 128], "bfloat16"),
    "kown": ("sbuf", [128, 128], "bfloat16"),
    "tabs": ("sbuf", [128, 2048], "bfloat16"),
    "ws": ("sbuf", [128, 512], "bfloat16"),
    "oa": ("sbuf", [128, 512], "bfloat16"), "ob": ("sbuf", [128, 512], "bfloat16"),
    "oo": ("sbuf", [128, 512], "bfloat16"), "op": ("sbuf", [128, 512], "bfloat16"),
    "ea": ("sbuf", [128, 512], "bfloat16"), "eb": ("sbuf", [128, 512], "bfloat16"),
    "eo": ("sbuf", [128, 512], "bfloat16"), "ep": ("sbuf", [128, 512], "bfloat16"),
    "ys": ("sbuf", [128, 128], "float32"),
    "tabq": ("sbuf", [128, 512], "float8_e4m3fn_x4"), "tabp": ("sbuf", [128, 512], "uint8"),
    "wq": ("sbuf", [128, 128], "float8_e4m3fn_x4"), "wp": ("sbuf", [128, 128], "uint8"),
    "oq": ("sbuf", [128, 512], "float8_e4m3fn_x4"), "opl": ("sbuf", [128, 512], "uint8"),
    "eq": ("sbuf", [128, 512], "float8_e4m3fn_x4"), "epl": ("sbuf", [128, 512], "uint8"),
    "lq": ("sbuf", [128, 384], "float8_e4m3fn_x4"), "lp": ("sbuf", [128, 384], "uint8"),
    "viaq": ("sbuf", [128, 128], "float8_e4m3fn_x4"), "viap": ("sbuf", [128, 128], "uint8"),
    "z": ("psum", [128, 4096], "float32"),
}
SEMAPHORES = [
    "l_ids", "l_tg", "l_tab0", "l_tab1", "l_w", "l_kp", "l_kr", "sent",
    "a_id0", "a_id1", "a_id2", "a_e0", "a_e1", "a_e2", "h_ids", "h_pl", "h_co",
    "pc", "m_k", "m_1", "m_g", "m_m", "m_c", "m_cf", "q_tab", "q_w", "kown", "yz", "yv", "stored", "w1", "w2",
] + ["%s%d" % (n, k) for n in ("tp", "tr") for k in range(5)] \
  + [n + t for t in "abop" for n in ("o_", "qo_", "es_", "ev_", "qe_")] \
  + ["z%s%d" % (t, f) for t in "abop" for f in range(4)]

_PLAN = {}
COL = {"a": 0, "b": 1, "o": 2, "p": 3}


def relays(T, topo):
    if _PLAN:
        return _PLAN
    taken = set(T.cores)
    for r in T.cores:
        for j in T.cores:
            if r == j or topo.may_write(r, j):
                continue
            switch_first = topo.die(r) == topo.die(j)
            for c in range(4 * topo.CORES_PER_HOST):
                if c in taken or topo.chip(c) != topo.chip(r) or topo.die(c) != topo.die(r):
                    continue
                if topo.host(c) in (topo.host(r), topo.host(j)):
                    continue
                if not (topo.may_write(r, c) and topo.may_write(c, j)):
                    continue
                if topo.same_plane(r, c) != switch_first:
                    continue
                _PLAN[(r, j)] = c
                taken.add(c)
                break
    return _PLAN


def engines(mask):
    return [1 << k for k in range(16) if mask & (1 << k)]


def diagonal(T, topo, core):
    return [c for c in T.cores if c != core and not topo.may_write(c, core)]


def rank_program(g, core, T, topo):
    plan = relays(T, topo)
    if T.rank_of(core) is not None:
        owner_program(g, core, T, topo, plan)
        return
    for (r, j), c in plan.items():
        if c == core:
            relay_program(g, core, T, topo, r, j)


def relay_program(g, core, T, topo, r, j):
    s = T.sem
    slot = diagonal(T, topo, j).index(r)
    rid, pid = topo.addr(j, core)
    full = topo.mask(core, j)
    eng = engines(full)
    n_in = len(engines(topo.mask(r, core)))
    cols = slice(slot * NC, slot * NC + NC)
    g.wait_ge(s.h_ids, 1)
    g.remote_dma(T.ids_in[slot], T.ids_via[:], s["a_id%d" % slot], s.sent, pid, rid, eng[0])
    g.wait_ge(s.h_co, n_in)
    g.remote_dma(T.lq[:, cols].bitcast(dt.uint8), T.viaq[:].bitcast(dt.uint8), s["a_e%d" % slot], s.sent, pid, rid, full)
    g.wait_ge(s.h_pl, n_in // 2)
    g.remote_dma(T.lp[:, cols], T.viap[:], s["a_e%d" % slot], s.sent, pid, rid, full)
    g.wait_ge(s.sent, 1 + 2 * len(eng))


def owner_program(g, core, T, topo, plan):
    s = T.sem
    V, A, P, S = g.vector, g.scalar, g.tensor, g.sync
    rank = T.rank_of(core)
    shift = -1024.0 * rank - 256.0
    diag = diagonal(T, topo, core)
    peer = [c for c in T.cores if c != core and c not in diag][0]
    slot = sorted(range(2), key=lambda k: 0 if topo.same_plane(core, plan[(core, diag[k])]) else 1)
    via = [plan[(core, diag[k])] for k in slot]
    off = topo.mask(core, via[0]) & topo.mask(core, via[1])
    eng = engines(off)
    part = [sum(eng[0::2]), sum(eng[1::2])]
    dst = []
    for c in via:
        rid, pid = topo.addr(c, core)
        dst.append(DstId(rid=rid, pnc=pid))
    prid, ppid = topo.addr(peer, core)
    n_off = len(eng)

    def blk(t):
        return slice(NC * COL[t], NC * COL[t] + NC)

    S.dma_start(T.ids_out[:], T.tg[0:1, :]).then_inc(s.l_ids, 16)
    A.dma_start(T.tgs[:], T.tg[:, :]).then_inc(s.l_tg, 16)
    S.dma_start(T.tabs[:, 0:1024], T.tab[:, 0:1024]).then_inc(s.l_tab0, 16)
    A.dma_start(T.tabs[:, 1024:2048], T.tab[:, 1024:2048]).then_inc(s.l_tab1, 16)
    S.dma_start(T.ws[:], T.w[:, :]).then_inc(s.l_w, 16)

    g.iota(T.pc[:], [[1, 4]], -256, 4, allow_small_or_imprecise_dtypes=True).then_inc(s.pc, 1)
    g.wait_ge(s.l_ids, 16)
    g.remote_dma_fused([RemoteDMATransfer(dst_ids=dst, dma_engine_mask=eng[0], remote_sem=s.h_ids,
                                          srcs=[T.ids_out[:]], dsts=[T.ids_via[:], T.ids_via[:]])], local_sem=s.sent)
    g.remote_dma(T.ids_in[2], T.ids_out[:], s.a_id2, s.sent, ppid, prid, off)

    for q, aa in ((S, (0, 1)), (A, (2, 3))):
        q.wait_ge(s.m_k, 2)
        q.wait_ge(s.a_id0, 1)
        q.wait_ge(s.a_id1, 1)
        for a in aa:
            q.dma_start(T.kr[32 * a:32 * a + 6, :], T.ids_in[0:2]).then_inc(s.l_kr, 16)
    S.wait_ge(s.a_id2, n_off)
    for a in range(4):
        S.dma_start(T.kp[32 * a:32 * a + 3, :], T.ids_in[2]).then_inc(s.l_kp, 16)

    V.memset(T.kr[:], 0.0).then_inc(s.m_k, 1)
    V.memset(T.kp[:], 0.0).then_inc(s.m_k, 1)
    V.memset(T.cf[:], 0.0).then_inc(s.m_c, 1)
    V.memset(T.msk[:], 1.0).then_inc(s.m_1, 1)
    V.memset(T.gk[:], 0.0).then_inc(s.m_g, 1)
    V.wait_ge(s.m_c, 1)
    for c0, v in ((1, 256.0), (2, 4.0), (4, 256.0), (5, 4.0)):
        V.memset(T.cf[:, c0:128:32], v).then_inc(s.m_cf, 1)
    V.wait_ge(s.m_1, 1)
    V.memset(T.msk[:, 0:256:32], 0.0).then_inc(s.m_m, 1)
    V.wait_ge(s.l_tg, 16)
    V.tensor_scalar(T.u1[:], T.tgs[:, 0:128], 1024.0, shift, OP.mult, OP.add).then_inc(s.w1, 1)
    V.tensor_scalar(T.u2[:], T.tgs[:, 128:256], 4.0, None, OP.mult).then_inc(s.w1, 1)
    V.wait_ge(s.w1, 2)
    V.tensor_tensor(T.u3[:], T.u2[:], T.tgs[:, 256:384], OP.add).then_inc(s.w2, 1)
    V.wait_ge(s.w2, 1)
    V.tensor_tensor(T.kown[:], T.u3[:], T.u1[:], OP.add).then_inc(s.kown, 1)
    V.wait_ge(s.kown, 1)
    V.wait_ge(s.pc, 1)

    def onehot(t, tile, key):
        for f in range(4):
            V.tensor_scalar(tile[:, f:512:4], key, T.pc[:, f:f + 1], None, OP.is_equal).then_inc(s["o_" + t], 1)
        V.wait_ge(s["o_" + t], 4)
        V.quantize_mx(T.oq[:, blk(t)], T.opl[:, blk(t)], tile[:]).then_inc(s["qo_" + t], 1)

    onehot("o", T.oo, T.kown[:])
    for f in range(4):
        if f % 2 == 0:
            V.wait_ge(s["l_tab%d" % (f // 2)], 16)
        V.quantize_mx(T.tabq[:, NC * f:NC * f + NC], T.tabp[:, NC * f:NC * f + NC],
                      T.tabs[:, 512 * f:512 * f + 512]).then_inc(s.q_tab, 1)
    V.wait_ge(s.l_w, 16)
    V.quantize_mx(T.wq[:], T.wp[:], T.ws[:]).then_inc(s.q_w, 1)
    V.wait_ge(s.m_g, 1)
    V.wait_ge(s.m_m, 1)
    V.wait_ge(s.m_cf, 4)

    def keys(rows, cols, sc, base, n, out, t):
        V.transpose(cols[:], rows[:]).then_inc(s[t + "0"], 1)
        V.wait_ge(s[t + "0"], 1)
        V.tensor_tensor_scan(sc[:], T.cf[:], cols[:], 0.0, OP.mult, OP.add).then_inc(s[t + "1"], 1)
        V.wait_ge(s[t + "1"], 1)
        for k in range(n):
            b = base + 128 * k
            V.tensor_scalar(T.gk[:, b:b + 128:32], sc[:, 3 * k + 2:128:32], shift, None, OP.add).then_inc(s[t + "2"], 1)
        V.wait_ge(s[t + "2"], n)
        V.tensor_tensor_scan(T.rep[:, base:base + 128 * n], T.msk[:, 0:128 * n], T.gk[:, base:base + 128 * n], 0.0,
                             OP.mult, OP.add).then_inc(s[t + "3"], 1)
        V.wait_ge(s[t + "3"], 1)
        V.transpose(out[:], T.rep[:, base:base + 128 * n]).then_inc(s[t + "4"], 1)
        V.wait_ge(s[t + "4"], 1)

    def zbank(t, f):
        b = 512 * f + (0 if t in "ap" else 2048)
        return T.z[:, b:b + NC]

    def out_of_psum(t, tile, ff, on_vector):
        for f in ff:
            if on_vector:
                V.wait_ge(s["z%s%d" % (t, f)], 1)
                V.tensor_copy(tile[:, f:512:4], zbank(t, f)).then_inc(s["ev_" + t], 1)
            else:
                A.wait_ge(s["z%s%d" % (t, f)], 1)
                A.activation(tile[:, f:512:4], zbank(t, f), COPY).then_inc(s["es_" + t], 1)

    def copied(q, t):
        n_s = {"a": 3, "b": 2, "o": 4, "p": 2}[t]
        q.wait_ge(s["es_" + t], n_s)
        if n_s < 4:
            q.wait_ge(s["ev_" + t], 4 - n_s)

    def codes(t, tile):
        copied(V, t)
        V.quantize_mx(T.eq[:, blk(t)], T.epl[:, blk(t)], tile[:]).then_inc(s["qe_" + t], 1)

    V.wait_ge(s.l_kr, 64)
    keys(T.kr, T.fr, T.sr, 0, 2, T.kab, "tr")
    onehot("a", T.oa, T.kab[:, NC * slot[0]:NC * slot[0] + NC])
    onehot("b", T.ob, T.kab[:, NC * slot[1]:NC * slot[1] + NC])
    out_of_psum("a", T.ea, (3,), True)
    codes("a", T.ea)
    out_of_psum("b", T.eb, (1, 3), True)
    codes("b", T.eb)
    V.wait_ge(s.l_kp, 64)
    keys(T.kp, T.fp, T.sp, 256, 1, T.kpe, "tp")
    onehot("p", T.op, T.kpe[:])
    codes("o", T.eo)
    out_of_psum("p", T.ep, (1, 3), True)
    codes("p", T.ep)

    out_of_psum("o", T.eo, (0, 1, 2, 3), False)
    out_of_psum("a", T.ea, (0, 1, 2), False)
    out_of_psum("b", T.eb, (0, 2), False)
    out_of_psum("p", T.ep, (0, 2), False)

    P.wait_ge(s.q_tab, 4)
    for t, before in (("o", None), ("a", None), ("b", "o"), ("p", "a")):
        if before:
            copied(P, before)
        P.wait_ge(s["qo_" + t], 1)
        for f in range(4):
            P.matmul_mx(zbank(t, f), T.tabq[:, NC * f:NC * f + NC], T.tabp[:, NC * f:NC * f + NC],
                        T.oq[:, blk(t)], T.opl[:, blk(t)], True, True).then_inc(s["z%s%d" % (t, f)], 1)

    for k, t in ((0, "a"), (1, "b")):
        g.wait_ge(s["qe_" + t], 1)
        g.remote_dma(T.viaq[:].bitcast(dt.uint8), T.eq[:, blk(t)].bitcast(dt.uint8), s.h_co, s.sent, dst[k].pnc, dst[k].rid, off)
    g.remote_dma_fused([RemoteDMATransfer(dst_ids=[dst[k]], dma_engine_mask=part[k], remote_sem=s.h_pl,
                                          src=T.epl[:, blk(t)], dst=T.viap[:]) for k, t in ((0, "a"), (1, "b"))],
                       local_sem=s.sent)
    g.wait_ge(s.qe_p, 1)
    g.remote_dma(T.lq[:, 256:384].bitcast(dt.uint8), T.eq[:, blk("p")].bitcast(dt.uint8), s.a_e2, s.sent, ppid, prid, off)
    g.remote_dma(T.lp[:, 256:384], T.epl[:, blk("p")], s.a_e2, s.sent, ppid, prid, off)

    P.wait_ge(s.q_w, 1)
    copied(P, "b")
    P.wait_ge(s.qe_o, 1)
    yb = zbank("b", 0)
    P.matmul_mx(yb, T.wq[:], T.wp[:], T.eq[:, blk("o")], T.epl[:, blk("o")], True, False)
    for k in (2, slot[0], slot[1]):
        P.wait_ge(s["a_e%d" % k], 2 * n_off)
        mm = P.matmul_mx(yb, T.wq[:], T.wp[:], T.lq[:, NC * k:NC * k + NC], T.lp[:, NC * k:NC * k + NC], False, k == slot[1])
        if k == slot[1]:
            mm.then_inc(s.yz, 1)
    V.wait_ge(s.yz, 1)
    V.tensor_copy(T.ys[:], yb).then_inc(s.yv, 1)
    S.wait_ge(s.yv, 1)
    S.dma_start(T.y[:, :], T.ys[:]).then_inc(s.stored, 16)
    S.wait_ge(s.stored, 16)
    g.wait_ge(s.sent, 1 + n_off + 2 * n_off + n_off + 2 * n_off)
